import numpy as np, ml_dtypes
CORES = [3,11,19,27,35,43]
N = 6
BF = ml_dtypes.bfloat16
def gentries(a):
    return np.ascontiguousarray(a.reshape(8, 16, -1).transpose(0, 2, 1)).reshape(8, -1)
def gtable(e):
    e = np.asarray(e); return np.ascontiguousarray(e.reshape(8, -1, 16).transpose(0, 2, 1)).reshape(128, -1).astype(np.int32)
V, G, L, SH, RO = 512, 112, 8192, 3, 2
W = V + (N - 1) * G; NV = N * V; TOP = 32640; END = 2 ** 23
def place(x, r):
    d = (r - x // V) % N
    return np.where(d == 0, x % V, V + (d - 1) * G + x % V)
def rising(x, n):
    x = np.sort(x, axis=-1); x[..., 1:] = np.where(x[..., 1:] == x[..., :-1], NV, x[..., 1:]); x = np.sort(x, axis=-1)
    return np.where((np.arange(4) < n[..., None]) & (x < NV), x, -1)
def counts(rng):
    return rng.choice(np.array([0, 1, 2, 2, 3, 3, 4]), (N, 8, 3, V))
def parts(rng, size, share, n):
    nets = rng.integers(0, W, (N, 8, 2 * V)); lv = np.zeros((N, 8, 3, V, 4), np.int64); r = np.arange(N)[:, None]
    for g in range(8):
        p = int(size[g])
        if p <= N * G // 2:
            x = rng.permutation(N * G)[:p]; pool = np.sort(x // G * V + x % G)
            nets[:, g] = np.where(rng.random((N, 2 * V)) < share, place(pool[rng.integers(0, p, (N, 2 * V))], r), nets[:, g])
        else:
            pool = np.sort(rng.permutation(NV)[:p])
        lv[:, g] = pool[rng.integers(0, p, (N, 3, V, 4))]
    tb = rng.integers(0, 65536, (N, 8, 3, V))
    return nets, rising(lv, n), tb, rng.integers(0, TOP + 1, (N, 8, 16, L)), rng.integers(0, 20001, (N, 8, 16, V))
def pack(nets, lv, tb, ce, rq):
    return {"fan": np.stack([gtable(x) for x in nets]), "cells": ce.reshape(N, 128, L).astype(np.float32).astype(BF), "req": rq.reshape(N, 128, V).astype(np.float32).astype(BF),
            "leaf0": np.ascontiguousarray(lv.transpose(0, 1, 2, 4, 3)).reshape(N, 8, 12 * V).astype(np.int32), "tab0": tb.reshape(N, 8, 3 * V).astype(np.int32)}
def setup_inputs(rng):
    return pack(*parts(rng, rng.permutation(np.array([4, 6, 8, 12, 20, 28, 200, NV])), 0.4, counts(rng)))
def setup_inputs_ties(rng):
    nets, lv, tb, ce, rq = parts(rng, rng.permutation(np.array([4, 5, 6, 8, 10, 12, 16, 24])), 0.5, counts(rng))
    ce = 256 * rng.integers(0, 3, ce.shape); rq = 256 * rng.integers(0, 2, rq.shape)
    g = rng.permutation(8); ce[:, g[0]] = 1024; rq[:, g[0]] = 0
    for i in (1, 2): ce[:, g[i]] = rng.integers(0, 2, ce[:, g[i]].shape); rq[:, g[i]] = 0
    rq = np.where(rng.random((N, 8, 1, V)) < 0.1, TOP, rq)
    return pack(nets, lv, tb, ce, rq)
def setup_inputs_bare(rng):
    n = counts(rng); n[:, ::2] = 0; n[:, 5] = rng.integers(0, 2, (N, 3, V)); n[rng.integers(0, N)] = 0
    nets, lv, tb, ce, rq = parts(rng, rng.permutation(np.array([4, 6, 8, 12, 20, 28, 200, NV])), 0.4, n)
    nets[:, 1] = np.tile(np.arange(V), 2); nets[:, 3, V:] = nets[:, 3, :V]; nets[:, 4, V::2] = nets[:, 4, :V:2]
    return pack(nets, lv, tb, ce, rq)
def setup_inputs_ends(rng):
    nets, lv, tb, ce, rq = parts(rng, np.full(8, 8), 0.0, counts(rng))
    for g in range(8):
        p = (4, 5, 6, 8)[g % 4]
        pool = np.sort(np.concatenate([np.array([0, NV - 1]), 1 + rng.permutation(NV - 2)[:p - 2]]))
        lv[:, g] = rising(pool[np.argsort(rng.random((N, 3, V, p)), axis=-1)[..., :4]], np.full((N, 3, V), 4))
        if g % 2 == 1: nets[:, g] = rng.choice(np.array([0, V - 1, V, W - 1]), (N, 2 * V))
    tb = np.where(rng.random(tb.shape) < 0.6, rng.choice(np.array([0, 65535, 1, 32768, 43690, 65534]), tb.shape), tb)
    ce = np.where(rng.random(ce.shape) < 0.4, TOP * rng.integers(0, 2, ce.shape), ce); ce[:, :, :, 0] = rng.integers(0, TOP + 1, (N, 8, 16)); ce[:, 7] = np.where(rng.random((N, 16, L)) < 0.98, TOP, ce[:, 7])
    rq = np.where(rng.random(rq.shape) < 0.2, rng.choice(np.array([0, 1, TOP]), rq.shape), rq); rq = np.where(rng.random((N, 8, 1, V)) < 0.1, 0, rq)
    return pack(nets, lv, tb, ce, rq)
def setup_inputs_alike(rng):
    nets, lv, tb, ce, rq = parts(rng, rng.integers(3, 7, 8), 1.0, counts(rng))
    lv[:, ::2, 1:] = lv[:, ::2, :1]; tb[:, ::2, 1:] = tb[:, ::2, :1]
    return pack(nets, lv, tb, ce, rq)
def setup_inputs_spread(rng):
    nets, lv, tb, ce, rq = parts(rng, rng.permutation(np.array([4, 6, 8, 12, 20, 28, 200, NV])), 0.4, counts(rng))
    ce = np.minimum(np.floor(np.exp2(15 * rng.random((N, 8, 1, L))) * rng.random((N, 8, 16, L))), TOP)
    rq = np.minimum(np.floor(np.exp2(15 * rng.random((N, 8, 1, V))) * rng.random((N, 8, 16, V))), TOP)
    w = rng.random(tb.shape); t2 = rng.integers(0, 65536, tb.shape); t3 = rng.integers(0, 65536, tb.shape)
    tb = np.where(w < 0.3, tb & t2 & t3, np.where(w < 0.6, tb | t2 | t3, tb))
    nets[:, ::2] = np.where(rng.random((N, 4, 2 * V)) < 0.5, np.floor(W * rng.random((N, 4, 2 * V)) ** 3).astype(np.int64), nets[:, ::2])
    return pack(nets, lv, tb, ce, rq)
def check_inputs(d):
    bad = []
    for k, lo, hi in (("fan", 0, W - 1), ("cells", 0, TOP), ("req", 0, TOP), ("leaf0", -1, NV - 1), ("tab0", 0, 65535)):
        x = np.asarray(d[k]).astype(np.float32)
        if not (np.all(x >= lo) and np.all(x <= hi) and np.all(np.floor(x) == x)): bad.append("range of " + k)
    x = np.asarray(d["leaf0"]).reshape(-1, 4, V); a, b = x[:, :-1], x[:, 1:]
    if not np.all((b == -1) | ((a >= 0) & (b > a))): bad.append("order of leaf0")
    return bad
def old_rows():
    o = np.zeros((16, 16), np.int32)
    for s in range(16):
        k = 0
        for p in range(4):
            if (s >> p) & 1:
                o[s] |= (((np.arange(16) >> p) & 1) << k).astype(np.int32); k += 1
    return o
OLD = old_rows()
def turned(x, u, t):
    p = np.sum(u[..., None, :] < x[..., :, None], axis=-1)
    s = np.sum(np.where((x < NV) & (p < 4), 1 << np.minimum(p, 3), 0), axis=-1)
    return (t[..., None] >> OLD[s]) & 1
def reference(fan, cells, req, leaf0, tab0):
    lv = leaf0.astype(np.int32).reshape(N, 8, 3, 4, V).transpose(0, 1, 2, 4, 3); lv = np.where(lv < 0, np.int32(NV), lv)
    tb = tab0.astype(np.int32).reshape(N, 8, 3, V); co = np.full((N, 8, 3, V), -1, np.int32)
    nets = np.stack([gentries(x) for x in fan]).astype(np.int64).reshape(N, 8, 2, V)
    ce = cells.astype(np.float32).astype(np.int32).reshape(N, 8, 16, L); rq = req.astype(np.float32).astype(np.int32).reshape(N, 8, 16, V)
    own = np.full((N, 8, 1, V, 4), NV, np.int32); own[..., 0] = np.arange(NV, dtype=np.int32).reshape(N, 1, 1, V)
    triv = np.full((N, 8, 1, V), 43690, np.int32); bits = np.arange(16, dtype=np.int32)
    for rnd in range(RO):
        al = np.concatenate([lv, own], axis=2); at = np.concatenate([tb, triv], axis=2)
        lv = np.full_like(lv, NV); tb = np.zeros_like(tb); co = np.full_like(co, -1)
        for r in range(N):
            wl = np.concatenate([al[r]] + [al[(r - d) % N][:, :, :G] for d in range(1, N)], axis=2)
            wt = np.concatenate([at[r]] + [at[(r - d) % N][:, :, :G] for d in range(1, N)], axis=2)
            ia = nets[r, :, 0][:, None, :]; ib = nets[r, :, 1][:, None, :]
            xa = np.repeat(np.take_along_axis(wl, ia[..., None], 2), 4, axis=1); ta = np.repeat(np.take_along_axis(wt, ia, 2), 4, axis=1)
            xb = np.tile(np.take_along_axis(wl, ib[..., None], 2), (1, 4, 1, 1)); tc = np.tile(np.take_along_axis(wt, ib, 2), (1, 4, 1))
            both = np.sort(np.concatenate([xa, xb], axis=-1), axis=-1)
            both[..., 1:] = np.where(both[..., 1:] == both[..., :-1], np.int32(NV), both[..., 1:]); both = np.sort(both, axis=-1)
            u = both[..., :4]; void = (both[..., 4] < NV) | (xa[..., 0] == NV) | (xb[..., 0] == NV)
            t = (65535 - np.sum((turned(xa, u, ta) & turned(xb, u, tc)) << bits, axis=-1)).astype(np.int32)
            c1 = ((t + 29 * (t >> 5)) & (L - 1)).reshape(8, 1, 16 * V); c2 = (t >> SH).reshape(8, 1, 16 * V)
            e = np.minimum(np.take_along_axis(ce[r], c1, 2), np.take_along_axis(ce[r], c2, 2)).reshape(8, 16, 16, V)
            cost = np.sum(np.maximum(e - rq[r][:, :, None, :], 0), axis=1)
            key = np.where(void, END, 16 * cost + np.arange(16)[None, :, None])
            for c in range(3):
                k = np.min(key, axis=1); full = k < END; i = (k & 15)[:, None, :]
                lv[r, :, c] = np.where(full[..., None], np.take_along_axis(u, i[..., None], 1)[:, 0], NV)
                tb[r, :, c] = np.where(full, np.take_along_axis(t, i, 1)[:, 0], 0); co[r, :, c] = np.where(full, k >> 4, -1)
                key = np.where((key >> 4) == (k >> 4)[:, None, :], END, key)
    yl = np.where(lv == NV, -1, lv).transpose(0, 1, 2, 4, 3)
    return {"yl": np.ascontiguousarray(yl).reshape(N, 8, 12 * V).astype(np.float32), "yt": tb.reshape(N, 8, 3 * V).astype(np.float32), "yc": co.reshape(N, 8, 3 * V).astype(np.float32)}

import numpy as np
from concourse.bass import DstId, RemoteDMATransfer
from concourse.mybir import AluOpType as Alu, ActivationFunctionType as Act

S = np.s_
N, V, GB, WN = 6, 512, 112, 1072
F32, BF, F16, I32, U16 = "float32", "bfloat16", "float16", "int32", "uint16"
SIZE = {F32: 4, BF: 2, F16: 2, I32: 4, U16: 2}


def sb(shape, d):
    return ("sbuf", [128] + list(shape), d)


def ps(*shape):
    return ("psum", [128] + list(shape), F32)


SCRATCH = {
    "rot0": ps(4, 128), "rot1": ps(4, 128), "cd0": ps(4, 8, 4, 4), "cd1": ps(4, 8, 4, 4),
    "cod": ps(4, 128), "pk": ps(4, 128), "misc": ps(4, 8, 4, 4), "rr": ps(512),
    "cel0": sb([14144], BF), "cel1": sb([14144], BF), "rq": sb([512], BF),
    "fani": sb([2, 4, 16], I32), "off": sb([2, 3, 32], U16),
    "win0": sb([3 * WN], F32), "win1": sb([3 * WN], F32),
    "st": sb([2, 384], F32), "L16": sb([2, 512], F16), "G2": sb([2, 512], F32), "G3": sb([2, 512], BF),
    "ws0": sb([4104], F32), "ws1": sb([4104], F32),
    "sg": sb([2, 13, 128], BF), "ug": sb([2, 13, 128], BF), "bits": sb([2, 6, 128], BF),
    "fs": sb([2, 2, 128], BF), "vflag": sb([4, 128], BF),
    "ch": sb([2, 8, 4, 4], F32), "X": sb([2, 128], I32), "Y": sb([2, 2, 128], I32), "Z": sb([2, 128], I32),
    "Pq": sb([2, 128], I32), "N2": sb([2, 128], F32), "Hb": sb([2, 3, 128], BF),
    "c1": sb([4, 128], U16), "c2": sb([4, 128], U16), "Tsb": sb([2, 256], F32),
    "e2": sb([3, 1024], BF), "mm": sb([2, 2048], BF), "xx": sb([16, 128], BF),
    "M": sb([2, 3, 128], F32), "TH": sb([4, 3, 8], I32), "THR": sb([2, 128], F32), "bc": sb([128], F32),
    "fl": sb([128], F32), "K2": sb([2, 128], F32),
    "Mi": sb([2, 24], I32), "emp": sb([24], F32), "ix": sb([2, 24], F32), "ixu": sb([2, 128], U16),
    "ofs": sb([2, 24], U16), "sel": sb([384], F32), "U0": sb([32, 4, 4, 4], F32),
    "E1": sb([32, 4, 4], F32), "E2": sb([32, 2, 2, 4], F32), "E3": sb([32, 4, 4], BF),
    "t1": sb([32, 4, 3], F32), "t2": sb([32, 4, 3], F32), "t3": sb([32, 4, 3], F32), "t4": sb([32, 4, 3], F32),
    "i1": sb([5, 96], I32), "Tv": sb([32, 3], F32), "co": sb([4, 2, 12], F32), "ca": sb([2, 3, 8], F32),
    "rawT": sb([512], I32), "Y1": sb([2, 2, 128], F32), "Y2": sb([2, 2, 2, 128], F32),
    "it": sb([128], I32), "it2": sb([128], I32), "it3": sb([32], I32), "it4": sb([128], I32), "it5": sb([16], I32),
    "it7": sb([4], I32), "pc": sb([2], I32), "pb": sb([4, 2], I32), "pbf": sb([4, 2], F32), "col": sb([24], F32),
    "I32m": sb([4, 128], F32), "Ib": sb([12, 128], BF), "nI": sb([128], BF), "Pm": sb([128], F32),
    "Blk": sb([8, 16], F32), "EQ": sb([16], F32), "EQs": sb([2, 16], F32), "SelA": sb([13, 128], BF),
    "BW": sb([3, 8, 16], BF), "NA": sb([2, 8, 4, 4], BF), "Mj": sb([32], F32), "FW": sb([8, 3, 32], BF),
    "CF": sb([3, 8, 4, 4], BF), "CC": sb([2, 8, 8, 4, 4], BF), "IND": sb([128], BF), "one": sb([128], BF),
    "RW": sb([4, 8], F32), "fac": sb([2, 4, 8], F32), "wq": sb([2, 3, 8], F32), "EW": sb([8, 32], F16),
    "B8": sb([8], BF), "RQ": sb([128], BF), "PC": sb([128], BF), "RST": sb([128], F32), "NZ": sb([128], F32),
    "own": sb([32], F32),
}
IO = {"fan": [128, 64], "cells": [128, 8192], "req": [128, 512], "leaf0": [8, 6144], "tab0": [8, 1536],
      "yl": [8, 6144], "yt": [8, 1536], "yc": [8, 1536]}
SEMAPHORES = ["sV", "sS", "sP", "sG"] + ["r%s%d" % (a, i) for a in "al" for i in range(4)] + ["d%d" % i for i in range(60)]

PERM = [(0, 1, 2, 3), (0, 1, 3, 2), (0, 2, 3, 1), (0, 3, 1, 2), (1, 2, 3, 0), (1, 3, 0, 2), (2, 3, 1, 0), (3, 0, 1, 2)]
THS = [0, 1, 9, 18, 41, 50, 73, 105]
TRS = {0: 0, 4: 124, 6: 250, 7: 345}
AK, CUM, F0, TOFF = (32, 8, 2, 0), (10, 2, 0, 0), 30, 20
CY, PCY, LAT, GF, RLAT = 0.83e-3 * 1.2, 0.5e-3 * 1.2, 0.12, 1.55, 9.0
TRIES = 1200


def masks(ap):
    name, idx = ap
    sh = SCRATCH[name][1] if name in SCRATCH else IO[name]
    idx = idx if isinstance(idx, tuple) else (idx,)
    pm = np.zeros(sh[0], bool)
    pm[idx[0]] = True
    fm = np.zeros(sh[1:], bool)
    fm[idx[1:]] = True
    return pm, fm.reshape(-1)


def nfree(ap):
    return int(masks(ap)[1].sum())


def two(*aps):
    return all(SIZE[SCRATCH[a[0]][2]] == 2 for a in aps)


def banks(ap):
    return [ap[0]] if ap[0] in SCRATCH and SCRATCH[ap[0]][0] == "psum" else []


def isap(x):
    return isinstance(x, tuple)


def build():
    ops, stage = [], [0]

    def add(eng, ins, dur, lat=0.0, after=()):
        rd, wr = [], []
        for it in ins:
            wr += it[1]
            rd += it[2]
        ops.append({"rd": rd, "wr": wr, "dur": dur, "lat": lat, "alt": {eng: (ins, dur)}, "after": set(after), "stage": stage[0]})
        return len(ops) - 1

    def either():
        b = ops.pop()
        ops[-1]["alt"].update(b["alt"])

    def vd(n):
        return max(64, n) * CY + 0.03

    def ts(out, in0, s1, s2, o0, o1=None):
        add("V", [("ts", [out], [in0] + [x for x in (s1, s2) if isap(x)], (out, in0, s1, s2, o0, o1))],
            vd(nfree(out) * (0.5 if two(out, in0) else 1)))

    def ttin(out, a, b, o):
        return ("tt", [out], [a, b], (out, a, b, o)), vd(nfree(out) * (1 if banks(a) or banks(b) else 2))

    def tt(out, a, b, o):
        i, d = ttin(out, a, b, o)
        add("V", [i], d)

    def cp(out, a):
        add("V", [("cp", [out], [a], (out, a))], vd(nfree(out) * (0.5 if two(out, a) else 1)))

    def ms(out, c):
        add("V", [("ms", [out], [], (out, c))], vd(nfree(out) * (0.5 if two(out) else 1)))

    def scan(out, d0, d1, o0, o1):
        add("V", [("scan", [out], [d0, d1], (out, d0, d1, o0, o1))], vd(nfree(out)))

    def act(out, a, f, scale=1.0, bias=0.0):
        add("S", [("act", [out], [a] + [x for x in (scale, bias) if isap(x)], (out, a, f, scale, bias))], vd(nfree(out)))
        if f == Act.Identity:
            ts(out, a, scale, bias, Alu.mult, Alu.add)
        elif f == Act.Relu:
            ts(out, a, bias, 0.0, Alu.add, Alu.max)
        elif f == Act.Sign:
            ts(out, a, 1.0, -1.0, Alu.min, Alu.max)
        else:
            ts(out, a, 0.0, None, Alu.not_equal)
        either()

    def fill(out, c):
        ms(out, float(c))
        add("G", [("fill", [out], [], (out, int(c)))], 0.25 + 2 * nfree(out) * CY)
        either()

    def gat(eng, kind, out, win, off, *rest):
        ex = [x for x in rest if isap(x)]
        add(eng, [(kind, [out], [win, off] + ex, (out, win, off) + rest)], nfree(out) * GF * CY + 0.06)
        if kind == "gact":
            gat("V", "gcp", out, win, off)
            either()

    def mmg(lst):
        ins, d = [], 0.0
        for out, l, r, st, sp in lst:
            ins.append(("mm", [out], [l, r], (out, l, r, st, sp)))
            d += max(64, nfree(r)) * PCY * (4 if SCRATCH[l[0]][2] == F32 else 1)
        add("P", ins, d + 0.05)

    def grp(lst):
        return [(o, l, r, k == 0, k == len(lst) - 1) for k, (o, l, r) in enumerate(lst)]

    def iota(out, pat, base, cm):
        add("G", [("iota", [out], [], (out, pat, base, cm))], 0.25 + 2 * nfree(out) * CY)

    def dma(lst, lat=2.2, after=()):
        return add("Y", [("dma", [o], [a], (o, a)) for o, a in lst], 0.08 * len(lst), lat, after)

    rot, ring = [0], [0]

    def nrot():
        rot[0] ^= 1
        return "rot%d" % rot[0]

    AND, SHR = Alu.bitwise_and, Alu.logical_shift_right
    ID = Act.Identity
    LO, HI = slice(0, 64), slice(64, 128)

    def cells(X, k, after):
        return dma([(("cel%d" % X, S[h, 0:5952] if k else S[h, 5952:14144]), ("cells", S[64 * X:64 * X + 64, 2240 * k:8192]))
                    for h in (LO, HI)], 11.0, after)

    ms(("Y", S[:, :]), 0)
    first = [dma([(("Y", S[c::4]), ("leaf0", S[:, c * 2048:(c + 1) * 2048])) for c in range(3)]
                 + [(("rawT", S[0:24, :]), ("tab0", S[:, :]))])]
    first.append(dma([(("fani", S[h, X]), ("fan", S[64 * X:64 * X + 64, :])) for X in range(2) for h in (LO, HI)]
                     + [(("rq", S[64 * h:64 * h + 64, 256 * X:256 * X + 256]), ("req", S[64 * X:64 * X + 64, 256 * h:256 * h + 256]))
                        for X in range(2) for h in range(2)]))
    cells(0, 0, first)

    iota(("it", S[:, :]), [[-1, 128]], 0, 1)
    I1, IQ, IH = ("I32m", S[:, 0]), ("I32m", S[:, 1]), ("I32m", S[:, 2])
    ts(I1, ("it", S[:, :]), 0, None, Alu.is_equal)
    ts(IQ, ("it", S[:, :]), 0, 1.0 / 4096, Alu.is_equal, Alu.mult)
    act(IH, I1, ID, scale=-0.5)
    for X in range(2):
        add("G", [("own", [("own", S[:, 16 * X:16 * X + 16])], [], X)], 0.28)
    act(("E1", S[:, :, 0, 3]), ("own", S[:, :]), ID, scale=1.0 / 4096)
    act(("E2", S[:, :, 0, 0, 3]), ("own", S[:, :]), ID, scale=1.0 / 4096)
    act(("E2", S[:, :, 0, 1, 3]), ("own", S[:, :]), ID, scale=-1.0 / 4096, bias=4095.0 / 4096)
    fill(("E2", S[:, :, 1, :, 3]), 1)
    ms(("E3", S[:, :, :, :]), 0.0)
    IB = {}
    for k, val in enumerate([1, -2048, 1856, -8192, 29] + [65536 * s for s in (-5, -4, -3, -2, -1, 1, 2)]):
        IB[val] = ("Ib", S[:, k])
        act(IB[val], I1, ID, scale=float(val))
    act(("nI", S[:, :]), I1, ID, scale=-4096.0)
    act(("I32m", S[:, 3]), I1, ID, scale=4096.0)
    iota(("it2", S[:, :]), [[-16, 8], [0, 16]], 0, 1)
    ts(("it2", S[:, :]), ("it2", S[:, :]), 0x7FFFFFF0, None, AND)
    ts(("Blk", S[:, :, :]), ("it2", S[:, :]), 0, None, Alu.is_equal)
    iota(("pc", S[:, :]), [[15, 2]], 0, 1)
    for k in range(4):
        ts(("pb", S[:, k]), ("pc", S[:, :]), k, 1, SHR, AND)
    cp(("pbf", S[:, :, :]), ("pb", S[:, :, :]))
    iota(("it5", S[:, :]), [[-1, 16]], 16, 1)
    ts(("it5", S[:, :]), ("it5", S[:, :]), 15, None, AND)
    ts(("EQ", S[:, :]), ("it5", S[:, :]), 0, None, Alu.is_equal)
    act(("EQs", S[:, 0]), ("EQ", S[:, :]), ID, scale=4096.0)
    act(("EQs", S[:, 1]), ("EQ", S[:, :]), ID, scale=-64.0)

    def eq(a):
        return ("EQ", S[:, a:a + 1])

    def col(a):
        return ("col", S[:, a:a + 1])

    def bit(k, w):
        return ("pbf", S[:, k, w:w + 1])

    TILES = [(k, c) for k in range(4) for c in range(3)] + [(0, 3)]
    for t, (k, c) in enumerate(TILES):
        act(("SelA", S[:, t]), ("Blk", S[:, :, :]), ID, scale=("EQs", S[:, 0, 4 * k + c:4 * k + c + 1]))
    for c in range(3):
        act(("BW", S[:, c, :, 0:8]), ("Blk", S[:, :, 0:8]), ID, scale=eq(4 + c))
        act(("BW", S[:, c, :, 8:16]), ("Blk", S[:, :, 0:8]), ID, scale=eq(c))
    fill(("NA", S[:, 0, :, 3, :]), 0)
    fill(("NA", S[:, 1, :, :, 3]), 0)
    for i in range(3):
        act(("NA", S[:, 0, :, i, :]), ("Blk", S[:, :, 0:4]), ID, scale=("EQs", S[:, 1, 4 * i + 7:4 * i + 8]))
        act(("NA", S[:, 1, :, :, i]), ("Blk", S[:, :, 0:4]), ID, scale=("EQs", S[:, 1, 4 * i + 7:4 * i + 8]))
    tt(col(7), eq(7), eq(11), Alu.add)
    ts(col(8), col(7), eq(15), -1.0, Alu.add, Alu.mult)
    act(col(1), col(8), ID, bias=1.0)
    act(col(11), bit(2, 0), ID, scale=-0.75, bias=1.0)
    act(col(12), bit(3, 0), ID, scale=-15.0, bias=16.0)
    tt(col(13), col(11), col(12), Alu.mult)
    ts(col(14), bit(2, 0), bit(3, 0), -0.25, Alu.mult, Alu.mult)
    tt(col(15), col(13), col(14), Alu.add)
    act(col(2), col(15), ID, scale=-1.0)
    act(col(16), bit(2, 0), ID, scale=-8.0, bias=10.0)
    act(col(17), bit(3, 0), ID, scale=-1.0, bias=1.0)
    ts(col(3), col(16), col(17), col(15), Alu.mult, Alu.add)
    act(col(18), bit(0, 0), ID, scale=-0.5, bias=1.0)
    act(col(19), bit(1, 0), ID, scale=-0.75, bias=1.0)
    act(col(20), bit(2, 0), ID, scale=-15.0 / 16, bias=1.0)
    ts(col(4), col(18), col(19), col(20), Alu.mult, Alu.mult)
    ts(col(6), col(4), 1.0, -2.0, Alu.is_lt, Alu.mult)
    act(col(21), col(4), ID, scale=-0.25, bias=-64.25)
    ts(col(22), col(4), 0.5, -0.95, Alu.is_equal, Alu.mult)
    ts(col(5), col(21), col(6), col(22), Alu.mult, Alu.add)
    iota(("it3", S[:, :]), [[-16, 8], [-1, 4]], 0, 1)
    ts(("it3", S[:, :]), ("it3", S[:, :]), 0x7FFFFFF3, None, AND)
    ts(("Mj", S[:, :]), ("it3", S[:, :]), 0, col(1), Alu.is_equal, Alu.mult)
    for k in range(4):
        for t in range(2):
            act(("FW", S[:, 2 * k + t, 0]), ("Mj", S[:, :]), ID, scale=AK[k] / 2.0 + (CUM[k] if t else 0))
            act(("FW", S[:, 2 * k + t, 1]), ("Mj", S[:, :]), ID, scale=col(2 + t))
            act(("FW", S[:, 2 * k + t, 2]), ("Mj", S[:, :]), ID, scale=float(t))
    for ta in range(2):
        for tb in range(2):
            si, sj = (slice(3, 4) if ta else slice(0, 3)), (slice(3, 4) if tb else slice(0, 3))
            na, nb = (1 if ta else 4), (1 if tb else 4)
            fill(("CF", S[0:32, 0, :, si, sj]), -sum(CUM[:na]) * nb + TOFF * ta - F0)
            fill(("CF", S[0:32, 1, :, si, sj]), -sum(CUM[:nb]) * na + TOFF * tb - F0)
            fill(("CF", S[0:32, 2, :, si, sj]), (1 if ta else -20) + (1 if tb else -20) - na * nb)
    for q, pi in enumerate(PERM):
        w = [1 << sum(((m >> k) & 1) << pi[k] for k in range(4)) for m in range(16)]
        corr = sum((128 if m % 8 == 1 else 129) * (w[m] - 2 * w[m - 1]) for m in range(16) if m % 8)
        todo = [(((q - 5) * F0 - sum(THS[:q + 1])) * 65536 - corr, slice(0, 3) if q in TRS else slice(0, 4))]
        if q in TRS:
            todo.append((((q - 5) * F0 - TRS[q] + 100) * 65536 + sum(w[1::2]), slice(3, 4)))
        for val, si in todo:
            for k, piece in enumerate(((val >> 16) << 16, val & 0xFF00, val & 0xFF)):
                fill(("CC", S[32 * k:32 * k + 32, 0, q, :, si, :]), piece)
    for j in range(4):
        act(("CC", S[0:96, 1, :, :, :, j]), ("CC", S[0:96, 0, :, :, 3 if j == 3 else 0, :]), ID)
    fill(("one", S[:, :]), 1)
    iota(("it7", S[:, 0:2]), [[0, 2]], 0, 1)
    ts(("it7", S[:, 0:2]), ("it7", S[:, 0:2]), 31, None, AND)
    ts(col(23), ("it7", S[:, 0:1]), 0, None, Alu.is_equal)
    act(("IND", S[:, :]), ("one", S[:, :]), ID, scale=col(23))
    for k in range(4):
        q = 0
        while q < 8:
            e = q
            while e < 8 and PERM[e][k] == PERM[q][k]:
                e += 1
            fill(("RW", S[:, k, q:e]), 2 ** (2 ** PERM[q][k]) - 1)
            q = e
    for w in range(2):
        for k in range(4):
            act(("fac", S[:, w, k]), ("RW", S[:, k]), ID, scale=bit(k, w), bias=1.0)
    tt(("wq", S[:, :, 0:2]), ("fac", S[:, :, 0:2]), ("fac", S[:, :, 2:4]), Alu.mult)
    tt(("wq", S[:, :, 2]), ("wq", S[:, :, 0]), ("wq", S[:, :, 1]), Alu.mult)
    act(("wq", S[:, 1, 0]), ("wq", S[:, 1, 2]), ID, scale=col(6))
    tt(("wq", S[:, 0, 0]), ("wq", S[:, 0, 2]), ("wq", S[:, 1, 0]), Alu.add)
    for q in range(8):
        ts(("EW", S[:, q]), ("Blk", S[:, :, 0:4]), ("wq", S[:, 0, 0, q:q + 1]), None, Alu.mult)
    act(("B8", S[:, :]), ("Blk", S[:, :, 0]), ID, scale=2.0 ** -19)
    act(("RQ", S[:, :]), ("Blk", S[:, :, :]), ID, scale=-(2.0 ** -19))
    iota(("it4", S[:, :]), [[0, 8], [1, 16]], 0, 0)
    ts(("PC", S[:, :]), ("it4", S[:, :]), 2.0 ** -23, None, Alu.mult)
    ts(("NZ", S[:, :]), ("it4", S[:, :]), 0, None, Alu.not_equal)
    act(("RST", S[:, :]), ("NZ", S[:, :]), ID, scale=-32.0, bias=32.0)
    fill(("THR", S[:, :, :]), 0)
    iota(("it4", S[:, :]), [[1, 16], [16, 8]], 0, -1)
    ts(("Pm", S[:, :]), ("it4", S[:, :]), 0, None, Alu.is_equal)
    iota(("it7", S[:, 2:4]), [[128, 2]], 0, 1)
    cp(("col", S[:, 9:11]), ("it7", S[:, 2:4]))
    for X in range(2):
        ts(("ws%d" % X, S[:, 4096:4104]), ("Blk", S[:, 0, 0:8]), 0.0, eq(2), Alu.mult, Alu.is_equal)
        for w in range(3):
            for h in range(2):
                ts(("off", S[64 * h:64 * h + 64, X, w]), ("fani", S[64 * h:64 * h + 64, X, h::2]), 3.0, float(w), Alu.mult, Alu.add)
    act(("rr", S[:, :]), ("rq", S[:, :]), ID)

    def counts(gs):
        ts(("t4", S[:, gs, 1:4]), ("E1", S[:, gs, 1:4, 0:3]), 1.0, 1.0 / 64, Alu.is_ge, Alu.mult)
        ts(("t4", S[:, gs, 0]), ("E1", S[:, gs, 0, 0:3]), 1.0, -7.0 / 64, Alu.is_ge, Alu.mult)
        tt(("t3", S[:, gs, 0:2]), ("t4", S[:, gs, 0:2]), ("t4", S[:, gs, 2:4]), Alu.add)
        tt(("E1", S[:, gs, 1:4, 3]), ("t3", S[:, gs, 0]), ("t3", S[:, gs, 1]), Alu.add)

    sent, came, read = {}, {}, {}

    def send(ph):
        w = "win%d" % (ph & 1)
        if ph == 1 and 0 not in read:
            return
        sent[ph] = add("G", [("send", [], [(w, S[:, 0:3 * GB])], ph)], 1.0, RLAT, read.get(ph - 1, []) + ([came[ph - 1]] if ph > 1 else []))
        came[ph] = add("A", [("arrive", [(w, S[:, 3 * V:3 * WN])], [], ph)], 0.0, 1.0, [sent[ph]])

    def emit(ph, b):
        r, B, w = "pk", 2 * (ph & 1) + b, "win%d" % (ph & 1)
        g8 = slice(8 * B, 8 * B + 8)
        mmg([((r, S[:, 0]), ("E1", S[:, g8]), I1, True, True), ((r, S[:, 1]), ("E2", S[:, g8]), I1, True, True),
             ((r, S[:, 2]), ("E3", S[:, g8]), IB[1], True, True)])
        for k in range(3):
            act(("st", S[:, b, k::3]), (r, S[:, k]), ID)
        for h in range(2):
            dma([((w, S[t, 768 * h + 384 * b:768 * h + 384 * b + 384]), ("st", S[64 * h:64 * h + 64, b])) for t in (LO, HI)])
        if b == 0:
            send(ph)

    cp(("G2", S[:, 0]), ("Y", S[:, :]))
    cp(("G2", S[0:24, 1]), ("rawT", S[0:24, :]))
    for X in range(2):
        stage[0] += 1
        gs, fs = slice(16 * X, 16 * X + 16), slice(48 * X, 48 * X + 48)
        nodes = lambda b, h: slice(256 * h + 128 * b, 256 * h + 128 * b + 128)
        r = "pk"
        mmg([((r, S[:, b, 64 * h:64 * h + 64]), ("G2", S[:, 0, nodes(b, h)]), ("I32m", S[:, 1, 64 * X:64 * X + 64]), True, True)
             for b in range(2) for h in range(2)]
            + [((r, S[:, 2 + b, 12 * h:12 * h + 12]), ("G2", S[0:24, 1, nodes(b, h)]), ("I32m", S[0:24, 0, 12 * X:12 * X + 12]), True, True)
               for b in range(2) for h in range(2)])
        act(("U0", S[:, gs, :, 0, :]), (r, S[:, 0:2]), ID)
        cp(("i1", S[:, 0, fs]), (r, S[:, 2:4, 0:24]))
        x = lambda k: ("U0", S[:, gs, k, 0, 0:3])
        ts(("t1", S[:, gs]), x(slice(0, 4)), 0.0, None, Alu.is_lt)
        tt(("E1", S[:, gs, :, 0:3]), x(slice(0, 4)), ("t1", S[:, gs]), Alu.max)
        act(("E2", S[:, gs, :, 0, 0:3]), ("E1", S[:, gs, 0:2, 0:3]), ID)
        tt(("t2", S[:, gs, 0:2]), x(slice(0, 2)), x(slice(2, 4)), Alu.max)
        tt(("t3", S[:, gs, 2]), ("t2", S[:, gs, 0]), ("t2", S[:, gs, 1]), Alu.max)
        u = lambda k: ("U0", S[:, gs, k, 1, 0:3])
        tt(u(slice(0, 3)), x(slice(0, 3)), x(slice(1, 4)), Alu.min)
        tt(u(3), u(0), u(1), Alu.max)
        tt(("t3", S[:, gs, 3]), u(3), u(2), Alu.max)
        act(("E2", S[:, gs, :, 1, 0:3]), ("t3", S[:, gs, 2:4]), ID, scale=-1.0, bias=4095.0 / 4096)
        counts(gs)
        for k, (sh, mk) in enumerate(((0, 3), (0, 15), (0, 255), (8, 255))):
            ts(("i1", S[:, k + 1, fs]), ("i1", S[:, 0, fs]), sh, mk, SHR, AND)
        prev = ("i1", S[:, 1, fs])
        z = lambda k: ("U0", S[:, gs, k, 2, 0:3])
        for k, mul in ((1, 5.0), (2, 17.0), (3, 1.0)):
            if mul != 1.0:
                ts(z(0), prev, mul, None, Alu.mult)
                prev = z(0)
            tt(z(1), prev, ("i1", S[:, k + 1, fs]), Alu.subtract)
            tt(z(2), z(1), ("t1", S[:, gs, k]), Alu.mult)
            prev = {1: z(3), 2: ("E3", S[:, gs, 1, 0:3]), 3: ("E3", S[:, gs, 0, 0:3])}[k]
            tt(prev, z(2), ("i1", S[:, k + 1, fs]), Alu.add)
        emit(X, 0)
        emit(X, 1)
    late = cells(0, 1, [sent[0]])

    def fanin(ph):
        stage[0] += 1
        X = ph & 1
        w, ws = ("win%d" % X, S[:, :]), "ws%d" % X
        for s, lim in ((0, 1.0), (1, 0.5)):
            gat("V", "gts", ("L16", S[:, X, 256 * s:256 * s + 256]), w, ("off", S[:, X, 0, 16 * s:16 * s + 16]), -0.375, lim, Alu.add, Alu.min)
        gat("S", "gact", ("G3", S[:, X]), w, ("off", S[:, X, 2]))
        gat("S", "gact", ("G2", S[:, X]), w, ("off", S[:, X, 1]))
        read[ph] = list(range(len(ops) - 4, len(ops)))
        if ph == 0:
            send(1)
            cells(1, 1, [cells(1, 0, [late, sent[1]])])
        dma([((ws, S[0::4, 256 * p:256 * p + 256]), ("G2", S[p >> 2::4, X, 0:256])) for p in range(16)]
            + [((ws, S[f::4, 1024 * i:1024 * i + 1024]), ("G2", S[:, X, 256:512])) for i in range(4) for f in ((1, 2, 3) if ph < 2 else (1,))], 5.0)

    def logic(B):
        stage[0] += 1
        X, d = B >> 1, B & 1
        La, Lb = ("L16", S[:, X, 128 * d:128 * d + 128]), ("L16", S[:, X, 256 + 128 * d:384 + 128 * d])
        Ga = lambda s: ("G3", S[:, X, 256 * s + 128 * d:256 * s + 128 * d + 128])
        diff = lambda r, t: grp([((r, S[:, t % 4]), ("SelA", S[:, t]), La), ((r, S[:, t % 4]), ("nI", S[:, :]), Lb)])
        for t0 in (0, 4, 8):
            r = nrot()
            mmg(sum([diff(r, t) for t in range(t0, t0 + 4)], []))
            act(("sg", S[:, d, t0:t0 + 4]), (r, S[:, :, :]), Act.Sign)
            act(("ug", S[:, d, t0:t0 + 4]), ("sg", S[:, d, t0:t0 + 4]), Act.Abs)
        r = nrot()
        mmg(diff(r, 12) + [((r, S[:, 1 + c]), ("BW", S[:, c]), Ga(0), True, True) for c in range(3)])
        act(("sg", S[:, d, 12]), (r, S[:, 0]), Act.Sign)
        act(("bits", S[:, d, 0:3]), (r, S[:, 1:4]), ID, scale=col(4), bias=col(5))
        act(("ug", S[:, d, 12]), ("sg", S[:, d, 12]), Act.Abs)
        r = nrot()
        mmg([((r, S[:, c]), ("BW", S[:, c]), Ga(1), True, True) for c in range(3)])
        act(("bits", S[:, d, 3:6]), (r, S[:, 0:3]), ID, scale=col(4), bias=col(5))
        lst = [(("misc", S[:, 0:3]), ("one", S[0:1, :]), ("CF", S[0:1])),
               (("misc", S[:, 2]), La, ("NA", S[:, 0])), (("misc", S[:, 2]), Lb, ("NA", S[:, 1]))]
        for t, (k, c) in enumerate(TILES):
            lst.append((("misc", S[:, 0:3, :, c, :]), ("sg", S[:, d, t]), ("FW", S[:, 2 * k])))
            lst.append((("misc", S[:, 0:3, :, c, :]), ("ug", S[:, d, t]), ("FW", S[:, 2 * k + 1])))
        mmg(grp(lst))
        act(("fs", S[:, d]), ("misc", S[:, 0:2]), ID)
        act(("vflag", S[:, B]), ("misc", S[:, 2]), Act.Relu, bias=-4.0)
        stage[0] += 1
        for s in range(2):
            for b in range(2):
                cd, qs = "cd%d" % b, slice(4 * b, 4 * b + 4)
                lst = [((cd, S[:, :]), ("IND", S[0:65, :]), ("CC", S[0:65, s, qs]))]
                for q in range(4 * b, 4 * b + 4):
                    if q != 5:
                        lst.append(((cd, S[:, q & 3]), IB[65536 * (q - 5)], ("fs", S[:, d, s])))
                for c in range(3):
                    o = (cd, S[:, :, :, c, :]) if s == 0 else (cd, S[:, :, :, :, c])
                    lst.append((o, ("bits", S[:, d, 3 * s + c]), ("EW", S[:, qs])))
                mmg(grp(lst))
            act(("ch", S[:, s]), ("cd0", S[:, 0]), ID)
            for q in range(1, 8):
                si, sj = slice(0, 4 if s or q in TRS else 3), slice(0, 3 if s and q not in TRS else 4)
                tt(("X", S[:, s]) if q == 7 else ("ch", S[:, s, :, si, sj]), ("cd%d" % (q >> 2), S[:, q & 3, :, si, sj]),
                   ("ch", S[:, s, :, si, sj]), Alu.max)
        stage[0] += 1
        ts(("Y", S[:, :, 0]), ("X", S[:, :]), 0x5555, None, AND)
        ts(("Y", S[:, :, 1]), ("X", S[:, :]), 0xAAAA, None, AND)
        tt(("Z", S[:, :]), ("Y", S[:, 0]), ("Y", S[:, 1]), Alu.add)
        ts(("Pq", S[:, 0]), ("Z", S[:, 0]), 0xAAAA, None, AND)
        ts(("Pq", S[:, 1]), ("Z", S[:, 1]), 0x15554, None, AND)
        n2 = ("N2", S[:, d])
        tt(n2, ("Pq", S[:, 0]), ("Pq", S[:, 1]), Alu.add)
        P1, P2, P3 = ("cod", S[:, 0]), ("cod", S[:, 1]), ("cod", S[:, 2])
        H, Lq, H2 = ("Hb", S[:, d, 0]), ("Hb", S[:, d, 1]), ("Hb", S[:, d, 2])
        mmg([(P1, n2, IH, True, True)])
        act(H2, P1, ID, scale=1.0 / 2048, bias=129 + 64511.5 / 2048)
        act(H, P1, ID, scale=1.0 / 4096, bias=129 + 63487.5 / 4096)
        ts(("c2", S[:, B]), P1, 65531.5, 0.125, Alu.add, Alu.mult)
        act(("Tsb", S[:, X, 128 * d:128 * d + 128]), P1, ID, bias=65535.0)
        mmg(grp([(P2, n2, IH), (P2, IB[-2048], H2)]))
        act(Lq, P2, ID, scale=1.0 / 32, bias=129 + (65535 + 2048 * 129 - 15.5) / 32)
        mmg(grp([(P3, n2, IH), (P3, IB[1856], H2), (P3, IB[-8192], H), (P3, IB[29], Lq)]))
        ts(("c1", S[:, B]), P3, float(5952 + 65535 + (8192 - 1856 - 29) * 129), None, Alu.add)
        if d:
            dma([(("ws%d" % X, S[2::16, 0:4096]), ("Tsb", S[:, X]))])

    def cost(B):
        stage[0] += 1
        X, d = B >> 1, B & 1
        ce = "cel%d" % X
        for k in range(2):
            ring[0] = (ring[0] + 1) % 3
            gat("S", "gact", ("e2", S[:, ring[0]]), (ce, S[:, 5952:14144]), ("c2", S[:, B, 64 * k:64 * k + 64]))
            gat("V", "gtt", ("mm", S[:, d, 1024 * k:1024 * k + 1024]), (ce, S[:, :]), ("c1", S[:, B, 64 * k:64 * k + 64]),
                ("e2", S[:, ring[0]]), Alu.min)
        for p0 in range(0, 16, 4):
            l = [ttin(("xx", S[:, p]), ("rr", S[:, 128 * B:128 * B + 128]), ("mm", S[:, d, p::16]), Alu.max) for p in range(p0, p0 + 4)]
            add("V", [a for a, b in l], sum(b for a, b in l))
        stage[0] += 1
        K = ("cod", S[:, 3])
        lst = [(K, ("rq", S[:, 128 * B:128 * B + 128]), ("RQ", S[:, :])), (K, ("one", S[0:1, :]), ("PC", S[0:1, :])),
               (K, IB[1], ("vflag", S[:, B]))]
        for p in range(16):
            lst.append((("cod", S[:, 3, p::16]), ("xx", S[:, p]), ("B8", S[:, :])))
        mmg(grp(lst))
        for c in range(3):
            scan(("M", S[:, d, c]), ("RST", S[:, :]), K, Alu.max, Alu.min)
            if c < 2:
                ts(("TH", S[:, B, c]), ("M", S[:, d, c, 15::16]), 2.0 ** 19, -7.5 / 16, Alu.mult, Alu.add)
                ts(("THR", S[:, c, 0::16]), ("TH", S[:, B, c]), 2.0 ** -19, 2.0 ** -19, Alu.mult, Alu.add)
                scan(("bc", S[:, :]), ("NZ", S[:, :]), ("THR", S[:, c]), Alu.mult, Alu.add)
                tt(("fl", S[:, :]), K, ("bc", S[:, :]), Alu.is_lt)
                tt(("K2", S[:, c]), K, ("fl", S[:, :]), Alu.max)
                K = ("K2", S[:, c])

    def pick(ph, d):
        stage[0] += 1
        X = ph & 1
        B = 2 * X + d
        gs = slice(8 * B, 8 * B + 8)
        m = ("M", S[:, d, :, 15::16])
        ts(("Mi", S[:, 0]), m, 2.0 ** 23, None, Alu.mult)
        ts(("emp", S[:, :]), m, 1.0, 4096.0, Alu.is_ge, Alu.mult)
        ts(("Mi", S[:, 1]), ("Mi", S[:, 0]), 15, None, AND)
        ts(("ix", S[:, 0]), ("Mi", S[:, 1]), 256.0, col(9 + d), Alu.mult, Alu.add)
        tt(("ix", S[:, 1]), ("ix", S[:, 0]), ("emp", S[:, :]), Alu.max)
        if ph > 1:
            ts(("TH", S[:, B, 2]), ("M", S[:, d, 2, 15::16]), 2.0 ** 19, -7.5 / 16, Alu.mult, Alu.add)
            ts(("ca", S[:, 0]), m, 1.0, -(2.0 ** 24), Alu.is_ge, Alu.mult)
            tt(("ca", S[:, 1]), ("TH", S[:, B]), ("ca", S[:, 0]), Alu.add)
            for h in range(2):
                ts(("co", S[:, B, h]), ("ca", S[:, 1, :, 4 * h:4 * h + 4]), -1.0, None, Alu.max)
        r = "pk"
        mmg([((r, S[0:24, 3]), ("ix", S[:, 1]), ("Pm", S[:, :]), True, True)])
        cp(("ixu", S[0:24, d]), (r, S[0:24, 3]))
        dma([(("ofs", S[:, d, 8 * c:8 * c + 8]), ("ixu", S[8 * c:8 * c + 8, d])) for c in range(3)])
        gat("S", "gact", ("sel", S[:, :]), ("ws%d" % X, S[:, :]), ("ofs", S[:, d]))
        mmg([((r, S[:, c]), ("sel", S[:, 128 * c:128 * c + 128]), I1, True, True) for c in range(3)])
        for c in range(3):
            act(("U0", S[:, gs, :, :, c]), (r, S[:, c]), ID)
        X0, Y0, X1, Y1 = [("U0", S[:, gs, k:k + 2, s, 0:3]) for k, s in ((0, 0), (0, 1), (2, 0), (2, 1))]
        a, b = slice(0, 2), slice(2, 4)
        tt(("E2", S[:, gs, 0, :, 0:3]), X0, Y0, Alu.min)
        tt(("t1", S[:, gs, a]), X0, Y0, Alu.max)
        tt(("t1", S[:, gs, b]), X0, Y0, Alu.is_equal)
        tt(("t2", S[:, gs, a]), X1, Y1, Alu.min)
        tt(("t2", S[:, gs, b]), ("t1", S[:, gs, a]), ("t1", S[:, gs, b]), Alu.max)
        tt(("E2", S[:, gs, 1, :, 0:3]), ("t2", S[:, gs, a]), ("t2", S[:, gs, b]), Alu.min)
        act(("t3", S[:, gs, b]), ("E2", S[:, gs, :, 1, 0:3]), ID, scale=-1.0, bias=4095.0 / 4096)
        for k in range(2):
            tt(("t1", S[:, gs, k]), ("t3", S[:, gs, 2 + k]), ("E2", S[:, gs, 1, 0, 0:3]), Alu.is_le)
        tt(("t2", S[:, gs, a]), ("t3", S[:, gs, b]), ("t1", S[:, gs, a]), Alu.max)
        tt(("E1", S[:, gs, 2, 0:3]), ("t2", S[:, gs, 0]), ("t2", S[:, gs, 1]), Alu.min)
        tt(("E1", S[:, gs, 3, 0:3]), ("t3", S[:, gs, 2]), ("t1", S[:, gs, 1]), Alu.max)
        act(("E1", S[:, gs, 0:2, 0:3]), ("E2", S[:, gs, :, 0, 0:3]), ID)
        Tn = ("U0", S[:, gs, 0, 2, 0:3])
        if ph < 2:
            counts(gs)
            ts(("i1", S[:, 0, 0:24]), Tn, -127.5, 1.0 / 256, Alu.add, Alu.mult)
            cp(("E3", S[:, gs, 0, 0:3]), ("i1", S[:, 0, 0:24]))
            act(("Tv", S[:, gs]), ("E3", S[:, gs, 0, 0:3]), ID, scale=-256.0)
            tt(("E3", S[:, gs, 1, 0:3]), Tn, ("Tv", S[:, gs]), Alu.add)
            emit(ph + 2, d)
            return
        act(("Tv", S[:, gs]), Tn, ID)
        mmg([((r, S[0:12, h]), ("Tv", S[:, 8 * B + 4 * h:8 * B + 4 * h + 4]), I1, True, True) for h in range(2)]
            + [((r, S[0:12, 2 + h]), ("co", S[:, B, h]), I1, True, True) for h in range(2)])
        act(("Y2", S[0:12, :, :, d]), (r, S[0:12, :, :]), ID)
        ts(("t4", S[:, gs, :]), ("E1", S[:, gs, :, 0:3]), 1.0, -4097.0 / 4096, Alu.is_ge, Alu.mult)
        tt(("E1", S[:, gs, :, 0:3]), ("E1", S[:, gs, :, 0:3]), ("t4", S[:, gs, :]), Alu.add)
        px = slice(64 * X, 64 * X + 64)
        mmg([((r, S[px, h]), ("E1", S[:, 8 * B + 4 * h:8 * B + 4 * h + 4]), ("I32m", S[:, 3]), True, True) for h in range(2)])
        act(("Y1", S[px, :, d]), (r, S[px, 0:2]), ID)
        if d:
            gx = slice(4 * X, 4 * X + 4)
            dma([(("yc", S[gx, 512 * c:512 * c + 512]), ("Y2", S[4 * c:4 * c + 4, 1])) for c in range(3)]
                + [(("yt", S[gx, :]), ("Y2", S[0:12, 0]))])
            dma([(("yl", S[gx, 2048 * c:2048 * c + 2048]), ("Y1", S[64 * X + c:64 * X + 64:4])) for c in range(3)])

    fanin(0)
    logic(0)
    logic(1)
    for ph in range(4):
        B, nx = 2 * (ph & 1), 2 * ((ph + 1) & 1)
        cost(B)
        if ph < 3:
            fanin(ph + 1)
            logic(nx)
        cost(B + 1)
        pick(ph, 0)
        if ph < 3:
            logic(nx + 1)
        pick(ph, 1)
    return ops


def depend(ops):
    acc = {}
    for n, o in enumerate(ops):
        dep = set(o["after"])
        rd = [(a[0],) + masks(a) for a in o["rd"]]
        wr = [(a[0],) + masks(a) for a in o["wr"]]
        for nm, pm, fm in rd:
            for m, w, p2, f2 in acc.get(nm, []):
                if w and (pm & p2).any() and (fm & f2).any():
                    dep.add(m)
        for nm, pm, fm in wr:
            keep = []
            for ent in acc.get(nm, []):
                m, w, p2, f2 = ent
                if m != n and (pm & p2).any() and (fm & f2).any():
                    dep.add(m)
                    if not (p2 & ~pm).any() and not (f2 & ~fm).any():
                        continue
                keep.append(ent)
            acc[nm] = keep + [(n, True, pm, fm)]
        for nm, pm, fm in rd:
            acc.setdefault(nm, []).append((n, False, pm, fm))
        o["dep"] = dep
        o["bk"] = sorted(set(sum([banks(a) for a in o["rd"] + o["wr"]], [])))


def schedule(ops, par):
    n = len(ops)
    vpen, slack, noise = abs(par[0]) / 10, abs(par[1]) / 40, [par[2 + o["stage"]] for o in ops]
    succ = [[] for _ in ops]
    for k, o in enumerate(ops):
        for m in o["dep"]:
            succ[m].append(k)
    pri = [0.0] * n
    for k in range(n - 1, -1, -1):
        pri[k] = ops[k]["dur"] + ops[k]["lat"] + LAT + max([pri[m] for m in succ[k]] + [0.0])
    left = [len(o["dep"]) for o in ops]
    ready = [k for k in range(n) if left[k] == 0]
    free, bank, fin, base, eng, order = {}, {}, [0.0] * n, [0.0] * n, [None] * n, []
    while ready:
        st = {}
        for k in ready:
            o = ops[k]
            best = None
            for e, (ins, dur) in o["alt"].items():
                t = max(free.get(e, 0.0), base[k])
                for b in o["bk"]:
                    if b in bank and eng[bank[b]] != e:
                        t = max(t, fin[bank[b]] + LAT)
                v = t + dur + (vpen + dur if e == "V" and len(o["alt"]) > 1 else 0.0)
                if best is None or v < best[0]:
                    best = (v, t, e, dur)
            st[k] = best[1:]
        k0 = min(ready, key=lambda k: st[k][0])
        k = max([m for m in ready if st[m][1] == st[k0][1] and st[m][0] <= st[k0][0] + slack], key=lambda m: (pri[m] + noise[m], -m))
        t, e, dur = st[k]
        eng[k] = e
        order.append((k, e, set(bank[b] for b in ops[k]["bk"] if b in bank and eng[bank[b]] != e), t))
        for b in ops[k]["bk"]:
            bank[b] = k
        free[e] = t + dur
        fin[k] = t + dur + ops[k]["lat"]
        ready.remove(k)
        for m in succ[k]:
            base[m] = max(base[m], fin[k] + LAT)
            left[m] -= 1
            if left[m] == 0:
                ready.append(m)
    return max(fin), order


PLAN = {}


def plan():
    if not PLAN:
        ops = build()
        depend(ops)
        rng = np.random.RandomState(1)
        par = np.zeros(3 + ops[-1]["stage"])
        par[:2] = 3.0
        best = schedule(ops, par)
        for _ in range(TRIES):
            new = par + rng.randn(len(par)) * 8.0 * (rng.rand(len(par)) < 0.06)
            got = schedule(ops, new)
            if got[0] <= best[0]:
                par, best = new, got
        PLAN["ops"] = ops
        PLAN["total"], PLAN["order"] = best
    return PLAN["ops"], PLAN["order"]


def rank_program(g, core, T, topo):
    rank = T.rank_of(core)
    if rank is None:
        return
    ops, order = plan()
    Q = {"V": g.vector, "S": g.scalar, "P": g.tensor, "G": g, "Y": g.sync}
    A = lambda a: T[a[0]][a[1]] if isap(a) else a
    cnt = {"sV": 0, "sS": 0, "sP": 0, "sG": 0}
    done, seen, ndma = {}, {}, [0]
    peers = [T.cores[(rank + d) % N] for d in range(1, N)]
    common = [e for e in topo.engines(core, peers[0]) if all(e in topo.engines(core, p) for p in peers)]
    emask = sum(1 << e for e in common)

    def wait(e, sem, val):
        if seen.get((e, sem), 0) < val:
            Q[e].wait_ge(T.sem[sem], val)
            seen[(e, sem)] = val

    for k, e, bw, _ in order:
        ins = ops[k]["alt"][e][0]
        if e == "A":
            done[k] = ("ra%d" % ins[0][3], len(common) * (N - 1))
            continue
        need = {"sG": cnt["sG"]} if e == "G" else {}
        for m in ops[k]["dep"] | bw:
            s, v = done[m]
            if e != "P" or s != "sP":
                need[s] = max(need.get(s, 0), v)
        for s in sorted(need):
            wait(e, s, need[s])
        q = Q[e]
        if e == "Y":
            s = "d%d" % ndma[0]
            ndma[0] += 1
            for kind, wr, rd, a in ins:
                q.dma_start(A(a[0]), A(a[1])).then_inc(T.sem[s], 16)
            cnt[s] = 16 * len(ins)
            done[k] = (s, cnt[s])
            continue
        for j, (kind, wr, rd, a) in enumerate(ins):
            if kind == "send":
                w = T["win%d" % (a & 1)]
                ids, dsts = [], []
                for d, p in enumerate(peers):
                    rid, pid, _ = topo.addr(p)
                    ids.append(DstId(rid=rid, pnc=pid))
                    dsts.append(w[:, 3 * (V + GB * d):3 * (V + GB * (d + 1))])
                g.remote_dma_fused([RemoteDMATransfer(dst_ids=ids, dma_engine_mask=emask, remote_sem=T.sem["ra%d" % a],
                                                      src=w[:, 0:3 * GB], dsts=dsts)], local_sem=T.sem["rl%d" % a])
                done[k] = ("rl%d" % a, len(common))
                cnt["rl%d" % a] = len(common)
                cnt["ra%d" % a] = len(common) * (N - 1)
                continue
            if kind == "ts":
                if a[5] is None:
                    i = q.tensor_scalar(A(a[0]), A(a[1]), A(a[2]), None, a[4])
                else:
                    i = q.tensor_scalar(A(a[0]), A(a[1]), A(a[2]), A(a[3]), a[4], a[5])
            elif kind == "tt":
                i = q.tensor_tensor(A(a[0]), A(a[1]), A(a[2]), a[3])
            elif kind == "cp":
                i = q.tensor_copy(A(a[0]), A(a[1]))
            elif kind == "ms":
                i = q.memset(A(a[0]), a[1])
            elif kind == "scan":
                i = q.tensor_tensor_scan(A(a[0]), A(a[1]), A(a[2]), 0.0, a[3], a[4])
            elif kind == "act":
                i = q.activation(A(a[0]), A(a[1]), a[2], bias=A(a[4]), scale=A(a[3]))
            elif kind == "gact":
                i = q.activation(A(a[0]), A(a[1]).indirect(A(a[2])), Act.Identity)
            elif kind == "gcp":
                i = q.tensor_copy(A(a[0]), A(a[1]).indirect(A(a[2])))
            elif kind == "gts":
                i = q.tensor_scalar(A(a[0]), A(a[1]).indirect(A(a[2])), a[3], a[4], a[5], a[6])
            elif kind == "gtt":
                i = q.tensor_tensor(A(a[0]), A(a[1]).indirect(A(a[2])), A(a[3]), a[4])
            elif kind == "mm":
                i = q.matmul(A(a[0]), A(a[1]), A(a[2]), a[3], a[4])
            elif kind == "iota":
                i = q.iota(A(a[0]), a[1], a[2], a[3])
            elif kind == "fill":
                i = q.iota(A(a[0]), [[0, nfree(a[0])]], a[1], 0, allow_small_or_imprecise_dtypes=True)
            elif kind == "own":
                i = q.iota(T.own[:, 16 * a:16 * a + 16], [[128, 2], [256, 2], [0, 4]], V * rank, 1, allow_small_or_imprecise_dtypes=True)
            if e != "P" or j == len(ins) - 1:
                s = "s" + e
                cnt[s] += 1
                i.then_inc(T.sem[s], 1)
                done[k] = (s, cnt[s])
    for s in sorted(cnt):
        if cnt[s]:
            wait("G", s, cnt[s])
